import numpy as np
import ml_dtypes


def mxq(x, axis, fmt="e4m3"):
    dtype, down = {"e4m3": (ml_dtypes.float8_e4m3fn, 7), "e5m2": (ml_dtypes.float8_e5m2, 14)}[fmt]
    v = np.moveaxis(np.asarray(x, np.float32).astype(ml_dtypes.bfloat16).astype(np.float64), axis, -1)
    blocks = v.reshape(v.shape[:-1] + (-1, 32))
    amax = np.abs(blocks).max(-1, keepdims=True)
    byte = np.maximum(np.where(amax > 0, np.frexp(amax)[1] - 1 + 127, 0) - down, 1)
    scale = np.exp2(byte - 127.0)
    codes = (blocks / scale).astype(np.float32).astype(dtype).astype(np.float64)
    return np.moveaxis((codes * scale).reshape(v.shape), -1, axis)


WIDE = False


def mx_kscale(k):
    if not WIDE:
        return np.ones(k)
    levels = np.array([10, -10, 5, -5, 0])
    if k % 512:
        return np.exp2(np.random.permutation(np.resize(levels, k // 32))).repeat(32)
    a = np.empty((k // 512, 16))
    for p in range(k // 512):
        a[p, :8] = np.random.permutation(np.resize(levels, 8))
        for g in range(8):
            far = levels[np.abs(levels - a[p, g]) >= 10]
            a[p, g + 8] = far[np.random.randint(len(far))]
    return np.exp2(a.ravel()).repeat(32)


def f64(x):
    return np.asarray(x).astype(np.float64)


def striped(idx):
    return np.tile(idx.reshape(-1, 16).T, (8, 1)).astype(np.uint16)


def unstriped(offs):
    return offs[:16].T.reshape(-1).astype(np.int64)


def pack_weight(w):
    k, n = w.shape
    w = f64(np.asarray(w, np.float32).astype(ml_dtypes.bfloat16)).reshape(k // 32, 32, n)
    amax = np.abs(w).max(1)
    byte = np.clip(np.where(amax > 0, np.frexp(amax)[1] - 1 + 127 - 7, 1), 1, 254)
    scaled = (w * np.exp2(127.0 - byte)[:, None, :]).reshape(k, n).astype(np.float32)
    words = np.ascontiguousarray(scaled.reshape(k // 512, 128, 4, n).transpose(0, 1, 3, 2)).astype(ml_dtypes.float8_e4m3fn).view(np.uint8)
    return words, np.ascontiguousarray(byte.astype(np.uint8).reshape(k // 512, 16, n))


def unpack_weight(words, scales):
    g, p, n, _ = words.shape
    vals = np.ascontiguousarray(words).view(ml_dtypes.float8_e4m3fn).astype(np.float64) * np.repeat(np.exp2(scales.astype(np.float64) - 127.0), 8, axis=1)[..., None]
    return vals.transpose(0, 1, 3, 2).reshape(g * 512, n)


K, T, S, N, D, U, V = 512, 2048, 512, 128, 4, 512, 128
P = 2 ** 7


def setup_inputs():
    n = np.random.standard_normal
    s = mx_kscale(K)[:, None]
    packed_xT = pack_weight(n((K, T)) * s)
    return {
        "x_words": packed_xT[0],
        "x_scales": packed_xT[1],
        "w1": (n((K, N)) / np.sqrt(K) / s).astype(np.float32),
        "field": (np.tile(n(U) * 0.7, (P, 1))).astype(np.float32),
        "lam": (np.random.uniform(0.5, 1.5, (N, 1))).astype(np.float32),
        "beta": (-np.random.uniform(0.1, 0.35, (N, 1))).astype(np.float32),
        "coup": (np.tile(np.random.uniform(0.3, 1.2, U), (P, 1))).astype(np.float32),
        "step": (np.tile(n(U), (P, 1))).astype(np.float32),
        "offs": striped(np.random.permutation(T)[:S]),
        "src": striped(np.repeat(np.random.permutation(S)[:V], D)),
        "dst": striped(np.random.randint(0, S, U)),
    }


def reference(x_words, x_scales, w1, field, lam, beta, coup, step, offs, src, dst):
    xq = unpack_weight(x_words, x_scales)[:, unstriped(offs)]
    y = mxq(f64(w1), 0, "e4m3").T @ xq
    dg = y[:, unstriped(dst)] - y[:, unstriped(src)] + f64(field)[:1]
    de = dg + f64(lam)
    rate = (np.exp(f64(beta) * ((de) ** 2))) * f64(coup)[:1]
    rs = rate * f64(step)[:1]
    drift = rs.reshape(len(rs), -1, D).sum(axis=2)
    tot = rate.reshape(len(rate), -1, D).sum(axis=2)
    return drift / (tot + 0.2) + np.log(tot)

@@ -1,0 +1,139 @@
+from contextlib import ExitStack
+
+import concourse.mybir as mybir
+
+K, T, S, M, D = 512, 2048, 512, 128, 4
+V = S // D
+FLOPS = 2 * K * M * S
+
+F32 = mybir.dt.float32
+BF16 = mybir.dt.bfloat16
+I32 = mybir.dt.int32
+U32 = mybir.dt.uint32
+U16 = mybir.dt.uint16
+U8 = mybir.dt.uint8
+FP8X4 = mybir.dt.float8_e4m3fn_x4
+ACT = mybir.ActivationFunctionType
+ALU = mybir.AluOpType
+
+P = 128
+PACK = 4
+LIST_ROWS = 16
+SITE_CHUNK = 128
+HOP_CHUNK = 128
+SUM_CHUNK = 256
+
+
+def tile_picked_yrates_drift_p_kernel(
+    tc, x_words, x_scales, w1, field, lam, beta, coup, step, offs, src, dst, out
+):
+    nc = tc.nc
+    with ExitStack() as ctx:
+        pool = ctx.enter_context(tc.tile_pool(name="held", bufs=1))
+        psum = ctx.enter_context(tc.psum_pool(name="psum", bufs=1))
+
+        offs_t = pool.tile([P, S // LIST_ROWS], U16, name="offs_t")
+        src_t = pool.tile([P, S // LIST_ROWS], U16, name="src_t")
+        dst_t = pool.tile([P, S // LIST_ROWS], U16, name="dst_t")
+        words = pool.tile([P, T], U32, name="words", align_bytes=64)
+        scales = pool.tile([P, T], U8, name="scales", align_bytes=64)
+        w_raw = pool.tile([P, PACK, M], F32, name="w_raw")
+        field_t = pool.tile([P, S], F32, name="field_t")
+        coup_t = pool.tile([P, S], F32, name="coup_t")
+        step_t = pool.tile([P, S], F32, name="step_t")
+        lam_t = pool.tile([P, 1], F32, name="lam_t")
+        beta_t = pool.tile([P, 1], F32, name="beta_t")
+
+        nc.vector.memset(scales[:].bitcast(I32), 0)
+
+        nc.sync.dma_start(offs_t[:], offs)
+        nc.sync.dma_start(out=w_raw[:], in_=w1.rearrange("(p j) m -> p j m", j=PACK))
+        for q in range(4):
+            nc.sync.dma_start(
+                out=scales[32 * q : 32 * q + 4, :].bitcast(I32),
+                in_=x_scales[0, 4 * q : 4 * q + 4, :].bitcast(I32),
+            )
+        nc.sync.dma_start(
+            out=words[:].bitcast(I32),
+            in_=x_words[0].rearrange("p n t -> p (n t)").bitcast(I32),
+        )
+        nc.sync.dma_start(src_t[:], src)
+        nc.sync.dma_start(dst_t[:], dst)
+        nc.sync.dma_start(out=field_t[:], in_=field)
+        nc.sync.dma_start(out=coup_t[:], in_=coup)
+        nc.sync.dma_start(out=step_t[:], in_=step)
+        nc.gpsimd.dma_start(out=lam_t[:], in_=lam)
+        nc.gpsimd.dma_start(out=beta_t[:], in_=beta)
+
+        w_grouped = pool.tile([P, M, PACK], BF16, name="w_grouped", align_bytes=64)
+        w_codes = pool.tile([P, M], U32, name="w_codes", align_bytes=64)
+        w_scales = pool.tile([P, M], U8, name="w_scales", align_bytes=64)
+        nc.scalar.activation(out=w_grouped[:], in_=w_raw[:].rearrange("p j m -> p m j"), func=ACT.Copy)
+        picked_scales = pool.tile([P, S], U8, name="picked_scales", align_bytes=64)
+        nc.vector.tensor_copy(picked_scales[:], scales[:].indirect(offs_t[:]))
+        nc.vector.quantize_mx(
+            out=w_codes[:].bitcast(FP8X4),
+            scales=w_scales[:],
+            in_=w_grouped[:].rearrange("p m j -> p (m j)"),
+        )
+
+        picked_words = pool.tile([P, S], U32, name="picked_words", align_bytes=64)
+        y = pool.tile([P, S], F32, name="y")
+        for c0 in range(0, S, SITE_CHUNK):
+            cols = slice(c0, c0 + SITE_CHUNK)
+            entries = slice(c0 // LIST_ROWS, (c0 + SITE_CHUNK) // LIST_ROWS)
+            nc.vector.tensor_copy(picked_words[:, cols], words[:].indirect(offs_t[:, entries]))
+            acc = psum.tile([P, SITE_CHUNK], F32, name="acc%d" % (c0 // SITE_CHUNK))
+            nc.tensor.matmul_mx(
+                out=acc[:],
+                lhsT=w_codes[:].bitcast(FP8X4),
+                lhsT_scale=w_scales[:],
+                rhs=picked_words[:, cols].bitcast(FP8X4),
+                rhs_scale=picked_scales[:, cols],
+                start=True,
+                stop=True,
+            )
+            nc.scalar.activation(out=y[:, cols], in_=acc[:], func=ACT.Copy)
+
+        y_dst = pool.tile([P, S], F32, name="y_dst")
+        from_src = pool.tile([P, S], F32, name="from_src")
+        dg = pool.tile([P, S], F32, name="dg")
+        de_sq = pool.tile([P, S], F32, name="de_sq")
+        boltz = pool.tile([P, S], F32, name="boltz")
+        for c0 in range(0, S, HOP_CHUNK):
+            cols = slice(c0, c0 + HOP_CHUNK)
+            entries = slice(c0 // LIST_ROWS, (c0 + HOP_CHUNK) // LIST_ROWS)
+            nc.scalar.activation(out=y_dst[:, cols], in_=y[:].indirect(dst_t[:, entries]), func=ACT.Copy)
+            nc.vector.tensor_tensor(from_src[:, cols], y[:].indirect(src_t[:, entries]), field_t[:, cols], ALU.subtract)
+            nc.vector.tensor_tensor(dg[:, cols], y_dst[:, cols], from_src[:, cols], ALU.subtract)
+            nc.scalar.activation(out=de_sq[:, cols], in_=dg[:, cols], func=ACT.Square, bias=lam_t[:])
+            nc.scalar.activation(out=boltz[:, cols], in_=de_sq[:, cols], func=ACT.Exp, scale=beta_t[:])
+
+        rate = pool.tile([P, V, D], F32, name="rate")
+        rs = pool.tile([P, V, D], F32, name="rs")
+        rate_pairs = pool.tile([P, V, 2], F32, name="rate_pairs")
+        rs_pairs = pool.tile([P, V, 2], F32, name="rs_pairs")
+        tot = pool.tile([P, V], F32, name="tot")
+        den = pool.tile([P, V], F32, name="den")
+        drift = pool.tile([P, V], F32, name="drift")
+        inv = pool.tile([P, V], F32, name="inv")
+        mean_step = pool.tile([P, V], F32, name="mean_step")
+        log_tot = pool.tile([P, V], F32, name="log_tot")
+        result = pool.tile([P, V], F32, name="result")
+        rate_flat = rate[:].rearrange("p v d -> p (v d)")
+        rs_flat = rs[:].rearrange("p v d -> p (v d)")
+        for c0 in range(0, S, SUM_CHUNK):
+            cols = slice(c0, c0 + SUM_CHUNK)
+            vs = slice(c0 // D, (c0 + SUM_CHUNK) // D)
+            nc.vector.tensor_tensor(rate_flat[:, cols], boltz[:, cols], coup_t[:, cols], ALU.mult)
+            nc.vector.tensor_tensor(rate_pairs[:, vs, :], rate[:, vs, 0:2], rate[:, vs, 2:4], ALU.add)
+            nc.vector.tensor_tensor(rs_flat[:, cols], rate_flat[:, cols], step_t[:, cols], ALU.mult)
+            nc.vector.scalar_tensor_tensor(den[:, vs], rate_pairs[:, vs, 0], 0.2, rate_pairs[:, vs, 1], ALU.add, ALU.add)
+            nc.vector.tensor_tensor(tot[:, vs], rate_pairs[:, vs, 0], rate_pairs[:, vs, 1], ALU.add)
+            nc.vector.tensor_tensor(rs_pairs[:, vs, :], rs[:, vs, 0:2], rs[:, vs, 2:4], ALU.add)
+            nc.vector.reciprocal(inv[:, vs], den[:, vs])
+            nc.vector.tensor_tensor(drift[:, vs], rs_pairs[:, vs, 0], rs_pairs[:, vs, 1], ALU.add)
+            nc.vector.tensor_tensor(mean_step[:, vs], drift[:, vs], inv[:, vs], ALU.mult)
+        nc.scalar.activation(out=log_tot[:], in_=tot[:], func=ACT.Ln)
+        nc.vector.tensor_tensor(result[:], mean_step[:], log_tot[:], ALU.add)
+        nc.sync.dma_start(out=out, in_=result[:])

@@ -19,7 +19,7 @@ ALU = mybir.AluOpType
 P = 128
 PACK = 4
 LIST_ROWS = 16
-SITE_CHUNK = 128
+SITE_CHUNKS = (256, 128, 128)
 HOP_CHUNK = 128
 SUM_CHUNK = 256
 
@@ -30,6 +30,7 @@ def tile_picked_yrates_drift_p_kernel(
     nc = tc.nc
     with ExitStack() as ctx:
         pool = ctx.enter_context(tc.tile_pool(name="held", bufs=1))
+        ring = ctx.enter_context(tc.tile_pool(name="ring", bufs=2))
         psum = ctx.enter_context(tc.psum_pool(name="psum", bufs=1))
 
         offs_t = pool.tile([P, S // LIST_ROWS], U16, name="offs_t")
@@ -39,7 +40,7 @@ def tile_picked_yrates_drift_p_kernel(
         scales = pool.tile([P, T], U8, name="scales", align_bytes=64)
         w_raw = pool.tile([P, PACK, M], F32, name="w_raw")
         field_t = pool.tile([P, S], F32, name="field_t")
-        coup_t = pool.tile([P, S], F32, name="coup_t")
+        weights = pool.tile([P, 2, S], F32, name="weights")
         step_t = pool.tile([P, S], F32, name="step_t")
         lam_t = pool.tile([P, 1], F32, name="lam_t")
         beta_t = pool.tile([P, 1], F32, name="beta_t")
@@ -59,11 +60,11 @@ def tile_picked_yrates_drift_p_kernel(
         )
         nc.sync.dma_start(src_t[:], src)
         nc.sync.dma_start(dst_t[:], dst)
-        nc.sync.dma_start(out=field_t[:], in_=field)
-        nc.sync.dma_start(out=coup_t[:], in_=coup)
+        nc.sync.dma_start(out=weights[:, 0, :], in_=coup)
         nc.sync.dma_start(out=step_t[:], in_=step)
-        nc.gpsimd.dma_start(out=lam_t[:], in_=lam)
-        nc.gpsimd.dma_start(out=beta_t[:], in_=beta)
+        nc.sync.dma_start(out=field_t[:], in_=field)
+        nc.sync.dma_start(out=lam_t[:], in_=lam)
+        nc.sync.dma_start(out=beta_t[:], in_=beta)
 
         w_grouped = pool.tile([P, M, PACK], BF16, name="w_grouped", align_bytes=64)
         w_codes = pool.tile([P, M], U32, name="w_codes", align_bytes=64)
@@ -79,11 +80,12 @@ def tile_picked_yrates_drift_p_kernel(
 
         picked_words = pool.tile([P, S], U32, name="picked_words", align_bytes=64)
         y = pool.tile([P, S], F32, name="y")
-        for c0 in range(0, S, SITE_CHUNK):
-            cols = slice(c0, c0 + SITE_CHUNK)
-            entries = slice(c0 // LIST_ROWS, (c0 + SITE_CHUNK) // LIST_ROWS)
+        for i, width in enumerate(SITE_CHUNKS):
+            c0 = sum(SITE_CHUNKS[:i])
+            cols = slice(c0, c0 + width)
+            entries = slice(c0 // LIST_ROWS, (c0 + width) // LIST_ROWS)
             nc.vector.tensor_copy(picked_words[:, cols], words[:].indirect(offs_t[:, entries]))
-            acc = psum.tile([P, SITE_CHUNK], F32, name="acc%d" % (c0 // SITE_CHUNK))
+            acc = psum.tile([P, width], F32, name="acc%d" % i)
             nc.tensor.matmul_mx(
                 out=acc[:],
                 lhsT=w_codes[:].bitcast(FP8X4),
@@ -95,8 +97,9 @@ def tile_picked_yrates_drift_p_kernel(
             )
             nc.scalar.activation(out=y[:, cols], in_=acc[:], func=ACT.Copy)
 
+        nc.vector.tensor_tensor(weights[:, 1, :], weights[:, 0, :], step_t[:], ALU.mult)
+
         y_dst = pool.tile([P, S], F32, name="y_dst")
-        from_src = pool.tile([P, S], F32, name="from_src")
         dg = pool.tile([P, S], F32, name="dg")
         de_sq = pool.tile([P, S], F32, name="de_sq")
         boltz = pool.tile([P, S], F32, name="boltz")
@@ -104,36 +107,35 @@ def tile_picked_yrates_drift_p_kernel(
             cols = slice(c0, c0 + HOP_CHUNK)
             entries = slice(c0 // LIST_ROWS, (c0 + HOP_CHUNK) // LIST_ROWS)
             nc.scalar.activation(out=y_dst[:, cols], in_=y[:].indirect(dst_t[:, entries]), func=ACT.Copy)
-            nc.vector.tensor_tensor(from_src[:, cols], y[:].indirect(src_t[:, entries]), field_t[:, cols], ALU.subtract)
-            nc.vector.tensor_tensor(dg[:, cols], y_dst[:, cols], from_src[:, cols], ALU.subtract)
+            from_src = ring.tile([P, HOP_CHUNK], F32, name="from_src")
+            nc.vector.tensor_tensor(from_src[:], y[:].indirect(src_t[:, entries]), field_t[:, cols], ALU.subtract)
+            nc.vector.tensor_tensor(dg[:, cols], y_dst[:, cols], from_src[:], ALU.subtract)
             nc.scalar.activation(out=de_sq[:, cols], in_=dg[:, cols], func=ACT.Square, bias=lam_t[:])
             nc.scalar.activation(out=boltz[:, cols], in_=de_sq[:, cols], func=ACT.Exp, scale=beta_t[:])
 
-        rate = pool.tile([P, V, D], F32, name="rate")
-        rs = pool.tile([P, V, D], F32, name="rs")
-        rate_pairs = pool.tile([P, V, 2], F32, name="rate_pairs")
-        rs_pairs = pool.tile([P, V, 2], F32, name="rs_pairs")
-        tot = pool.tile([P, V], F32, name="tot")
+        terms = pool.tile([P, 2, V, D], F32, name="terms")
+        pairs = pool.tile([P, 2, V, 2], F32, name="pairs")
+        sums = pool.tile([P, 2, V], F32, name="sums")
         den = pool.tile([P, V], F32, name="den")
-        drift = pool.tile([P, V], F32, name="drift")
         inv = pool.tile([P, V], F32, name="inv")
         mean_step = pool.tile([P, V], F32, name="mean_step")
         log_tot = pool.tile([P, V], F32, name="log_tot")
         result = pool.tile([P, V], F32, name="result")
-        rate_flat = rate[:].rearrange("p v d -> p (v d)")
-        rs_flat = rs[:].rearrange("p v d -> p (v d)")
+        terms_flat = terms[:].rearrange("p s v d -> p s (v d)")
         for c0 in range(0, S, SUM_CHUNK):
             cols = slice(c0, c0 + SUM_CHUNK)
             vs = slice(c0 // D, (c0 + SUM_CHUNK) // D)
-            nc.vector.tensor_tensor(rate_flat[:, cols], boltz[:, cols], coup_t[:, cols], ALU.mult)
-            nc.vector.tensor_tensor(rate_pairs[:, vs, :], rate[:, vs, 0:2], rate[:, vs, 2:4], ALU.add)
-            nc.vector.tensor_tensor(rs_flat[:, cols], rate_flat[:, cols], step_t[:, cols], ALU.mult)
-            nc.vector.scalar_tensor_tensor(den[:, vs], rate_pairs[:, vs, 0], 0.2, rate_pairs[:, vs, 1], ALU.add, ALU.add)
-            nc.vector.tensor_tensor(tot[:, vs], rate_pairs[:, vs, 0], rate_pairs[:, vs, 1], ALU.add)
-            nc.vector.tensor_tensor(rs_pairs[:, vs, :], rs[:, vs, 0:2], rs[:, vs, 2:4], ALU.add)
+            nc.vector.tensor_tensor(
+                terms_flat[:, :, cols],
+                boltz[:, cols].unsqueeze(1).to_broadcast([P, 2, SUM_CHUNK]),
+                weights[:, :, cols],
+                ALU.mult,
+            )
+            nc.vector.tensor_tensor(pairs[:, :, vs, :], terms[:, :, vs, 0:2], terms[:, :, vs, 2:4], ALU.add)
+            nc.vector.scalar_tensor_tensor(den[:, vs], pairs[:, 0, vs, 0], 0.2, pairs[:, 0, vs, 1], ALU.add, ALU.add)
+            nc.vector.tensor_tensor(sums[:, :, vs], pairs[:, :, vs, 0], pairs[:, :, vs, 1], ALU.add)
             nc.vector.reciprocal(inv[:, vs], den[:, vs])
-            nc.vector.tensor_tensor(drift[:, vs], rs_pairs[:, vs, 0], rs_pairs[:, vs, 1], ALU.add)
-            nc.vector.tensor_tensor(mean_step[:, vs], drift[:, vs], inv[:, vs], ALU.mult)
-        nc.scalar.activation(out=log_tot[:], in_=tot[:], func=ACT.Ln)
+            nc.vector.tensor_tensor(mean_step[:, vs], sums[:, 1, vs], inv[:, vs], ALU.mult)
+        nc.scalar.activation(out=log_tot[:], in_=sums[:, 0, :], func=ACT.Ln)
         nc.vector.tensor_tensor(result[:], mean_step[:], log_tot[:], ALU.add)
         nc.sync.dma_start(out=out, in_=result[:])

from contextlib import ExitStack

import concourse.mybir as mybir

K, T, S, M, D = 512, 2048, 512, 128, 4
V = S // D
FLOPS = 2 * K * M * S

F32 = mybir.dt.float32
BF16 = mybir.dt.bfloat16
I32 = mybir.dt.int32
U32 = mybir.dt.uint32
U16 = mybir.dt.uint16
U8 = mybir.dt.uint8
FP8X4 = mybir.dt.float8_e4m3fn_x4
ACT = mybir.ActivationFunctionType
ALU = mybir.AluOpType

P = 128
PACK = 4
LIST_ROWS = 16
SITE_CHUNKS = (256, 128, 128)
HOP_CHUNK = 128
SUM_CHUNK = 256


def tile_picked_yrates_drift_p_kernel(
    tc, x_words, x_scales, w1, field, lam, beta, coup, step, offs, src, dst, out
):
    nc = tc.nc
    with ExitStack() as ctx:
        pool = ctx.enter_context(tc.tile_pool(name="held", bufs=1))
        ring = ctx.enter_context(tc.tile_pool(name="ring", bufs=2))
        psum = ctx.enter_context(tc.psum_pool(name="psum", bufs=1))

        offs_t = pool.tile([P, S // LIST_ROWS], U16, name="offs_t")
        src_t = pool.tile([P, S // LIST_ROWS], U16, name="src_t")
        dst_t = pool.tile([P, S // LIST_ROWS], U16, name="dst_t")
        words = pool.tile([P, T], U32, name="words", align_bytes=64)
        scales = pool.tile([P, T], U8, name="scales", align_bytes=64)
        w_raw = pool.tile([P, PACK, M], F32, name="w_raw")
        field_t = pool.tile([P, S], F32, name="field_t")
        weights = pool.tile([P, 2, S], F32, name="weights")
        step_t = pool.tile([P, S], F32, name="step_t")
        lam_t = pool.tile([P, 1], F32, name="lam_t")
        beta_t = pool.tile([P, 1], F32, name="beta_t")

        nc.vector.memset(scales[:].bitcast(I32), 0)

        nc.sync.dma_start(offs_t[:], offs)
        nc.sync.dma_start(out=w_raw[:], in_=w1.rearrange("(p j) m -> p j m", j=PACK))
        for q in range(4):
            nc.sync.dma_start(
                out=scales[32 * q : 32 * q + 4, :].bitcast(I32),
                in_=x_scales[0, 4 * q : 4 * q + 4, :].bitcast(I32),
            )
        nc.sync.dma_start(
            out=words[:].bitcast(I32),
            in_=x_words[0].rearrange("p n t -> p (n t)").bitcast(I32),
        )
        nc.sync.dma_start(src_t[:], src)
        nc.sync.dma_start(dst_t[:], dst)
        nc.sync.dma_start(out=weights[:, 0, :], in_=coup)
        nc.sync.dma_start(out=step_t[:], in_=step)
        nc.sync.dma_start(out=field_t[:], in_=field)
        nc.sync.dma_start(out=lam_t[:], in_=lam)
        nc.sync.dma_start(out=beta_t[:], in_=beta)

        w_grouped = pool.tile([P, M, PACK], BF16, name="w_grouped", align_bytes=64)
        w_codes = pool.tile([P, M], U32, name="w_codes", align_bytes=64)
        w_scales = pool.tile([P, M], U8, name="w_scales", align_bytes=64)
        nc.scalar.activation(out=w_grouped[:], in_=w_raw[:].rearrange("p j m -> p m j"), func=ACT.Copy)
        picked_scales = pool.tile([P, S], U8, name="picked_scales", align_bytes=64)
        nc.vector.tensor_copy(picked_scales[:], scales[:].indirect(offs_t[:]))
        nc.vector.quantize_mx(
            out=w_codes[:].bitcast(FP8X4),
            scales=w_scales[:],
            in_=w_grouped[:].rearrange("p m j -> p (m j)"),
        )

        picked_words = pool.tile([P, S], U32, name="picked_words", align_bytes=64)
        y = pool.tile([P, S], F32, name="y")
        for i, width in enumerate(SITE_CHUNKS):
            c0 = sum(SITE_CHUNKS[:i])
            cols = slice(c0, c0 + width)
            entries = slice(c0 // LIST_ROWS, (c0 + width) // LIST_ROWS)
            nc.vector.tensor_copy(picked_words[:, cols], words[:].indirect(offs_t[:, entries]))
            acc = psum.tile([P, width], F32, name="acc%d" % i)
            nc.tensor.matmul_mx(
                out=acc[:],
                lhsT=w_codes[:].bitcast(FP8X4),
                lhsT_scale=w_scales[:],
                rhs=picked_words[:, cols].bitcast(FP8X4),
                rhs_scale=picked_scales[:, cols],
                start=True,
                stop=True,
            )
            nc.scalar.activation(out=y[:, cols], in_=acc[:], func=ACT.Copy)

        nc.vector.tensor_tensor(weights[:, 1, :], weights[:, 0, :], step_t[:], ALU.mult)

        y_dst = pool.tile([P, S], F32, name="y_dst")
        dg = pool.tile([P, S], F32, name="dg")
        de_sq = pool.tile([P, S], F32, name="de_sq")
        boltz = pool.tile([P, S], F32, name="boltz")
        for c0 in range(0, S, HOP_CHUNK):
            cols = slice(c0, c0 + HOP_CHUNK)
            entries = slice(c0 // LIST_ROWS, (c0 + HOP_CHUNK) // LIST_ROWS)
            nc.scalar.activation(out=y_dst[:, cols], in_=y[:].indirect(dst_t[:, entries]), func=ACT.Copy)
            from_src = ring.tile([P, HOP_CHUNK], F32, name="from_src")
            nc.vector.tensor_tensor(from_src[:], y[:].indirect(src_t[:, entries]), field_t[:, cols], ALU.subtract)
            nc.vector.tensor_tensor(dg[:, cols], y_dst[:, cols], from_src[:], ALU.subtract)
            nc.scalar.activation(out=de_sq[:, cols], in_=dg[:, cols], func=ACT.Square, bias=lam_t[:])
            nc.scalar.activation(out=boltz[:, cols], in_=de_sq[:, cols], func=ACT.Exp, scale=beta_t[:])

        terms = pool.tile([P, 2, V, D], F32, name="terms")
        pairs = pool.tile([P, 2, V, 2], F32, name="pairs")
        sums = pool.tile([P, 2, V], F32, name="sums")
        den = pool.tile([P, V], F32, name="den")
        inv = pool.tile([P, V], F32, name="inv")
        mean_step = pool.tile([P, V], F32, name="mean_step")
        log_tot = pool.tile([P, V], F32, name="log_tot")
        result = pool.tile([P, V], F32, name="result")
        terms_flat = terms[:].rearrange("p s v d -> p s (v d)")
        for c0 in range(0, S, SUM_CHUNK):
            cols = slice(c0, c0 + SUM_CHUNK)
            vs = slice(c0 // D, (c0 + SUM_CHUNK) // D)
            nc.vector.tensor_tensor(
                terms_flat[:, :, cols],
                boltz[:, cols].unsqueeze(1).to_broadcast([P, 2, SUM_CHUNK]),
                weights[:, :, cols],
                ALU.mult,
            )
            nc.vector.tensor_tensor(pairs[:, :, vs, :], terms[:, :, vs, 0:2], terms[:, :, vs, 2:4], ALU.add)
            nc.vector.scalar_tensor_tensor(den[:, vs], pairs[:, 0, vs, 0], 0.2, pairs[:, 0, vs, 1], ALU.add, ALU.add)
            nc.vector.tensor_tensor(sums[:, :, vs], pairs[:, :, vs, 0], pairs[:, :, vs, 1], ALU.add)
            nc.vector.reciprocal(inv[:, vs], den[:, vs])
            nc.vector.tensor_tensor(mean_step[:, vs], sums[:, 1, vs], inv[:, vs], ALU.mult)
        nc.scalar.activation(out=log_tot[:], in_=sums[:, 0, :], func=ACT.Ln)
        nc.vector.tensor_tensor(result[:], mean_step[:], log_tot[:], ALU.add)
        nc.sync.dma_start(out=out, in_=result[:])
